import numpy as np
import ml_dtypes


def mxq(x, axis, fmt="e4m3"):
    dtype, down = {"e4m3": (ml_dtypes.float8_e4m3fn, 7), "e5m2": (ml_dtypes.float8_e5m2, 14)}[fmt]
    v = np.moveaxis(np.asarray(x, np.float32).astype(ml_dtypes.bfloat16).astype(np.float64), axis, -1)
    blocks = v.reshape(v.shape[:-1] + (-1, 32))
    amax = np.abs(blocks).max(-1, keepdims=True)
    byte = np.maximum(np.where(amax > 0, np.frexp(amax)[1] - 1 + 127, 0) - down, 1)
    scale = np.exp2(byte - 127.0)
    codes = (blocks / scale).astype(np.float32).astype(dtype).astype(np.float64)
    return np.moveaxis((codes * scale).reshape(v.shape), -1, axis)


WIDE = False


def mx_kscale(k):
    if not WIDE:
        return np.ones(k)
    levels = np.array([10, -10, 5, -5, 0])
    if k % 512:
        return np.exp2(np.random.permutation(np.resize(levels, k // 32))).repeat(32)
    a = np.empty((k // 512, 16))
    for p in range(k // 512):
        a[p, :8] = np.random.permutation(np.resize(levels, 8))
        for g in range(8):
            far = levels[np.abs(levels - a[p, g]) >= 10]
            a[p, g + 8] = far[np.random.randint(len(far))]
    return np.exp2(a.ravel()).repeat(32)


def f64(x):
    return np.asarray(x).astype(np.float64)


def striped(idx):
    return np.tile(idx.reshape(-1, 16).T, (8, 1)).astype(np.uint16)


def unstriped(offs):
    return offs[:16].T.reshape(-1).astype(np.int64)


def gelu(v):
    return 0.5 * v * (1.0 + np.tanh(np.sqrt(2.0 / np.pi) * (v + 0.044715 * v**3)))


K, T, E, C, H, N = 512, 1280, 10, 256, 512, 128


def by_expert(wq, xq):
    return np.concatenate([wq[e].T @ xq[:, e * C:(e + 1) * C] for e in range(E)], axis=1)


def setup_inputs():
    n = np.random.standard_normal
    s = mx_kscale(K)[:, None]
    u = mx_kscale(H)
    first = np.random.permutation(np.repeat(np.arange(E), T // E))
    second = (first + 1 + np.random.permutation(np.repeat(np.arange(E - 1), -(-T // (E - 1)))[:T])) % E
    while np.bincount(second, minlength=E).max() != T // E:
        load = np.bincount(second, minlength=E); hi, lo = int(load.argmax()), int(load.argmin())
        t = np.flatnonzero((second == hi) & (first != lo))[0]; second[t] = lo
    slot_token = np.empty(E * C, np.int64); pos = np.empty((2, T), np.int64); fill = np.zeros(E, np.int64)
    place = np.stack([np.random.permutation(C) for _ in range(E)])
    for r, deal in enumerate((first, second)):
        for t in np.random.permutation(T):
            e = deal[t]; j = e * C + place[e, fill[e]]; fill[e] += 1; slot_token[j] = t; pos[r, t] = j
    g = np.random.uniform(0.2, 0.8, T)
    w_slot = np.empty(E * C); w_slot[pos[0]] = g; w_slot[pos[1]] = 1.0 - g
    return {
        "xT": (n((K, T)) * s).astype(np.float32),
        "w1": (n((E, K, H)) / np.sqrt(K) / s[None]).astype(np.float32),
        "w3": (n((E, K, H)) / np.sqrt(K) / s[None] * u[None, None, :]).astype(np.float32),
        "w2": (n((E, H, N)) / np.sqrt(H) / u[None, :, None]).astype(np.float32),
        "gate": np.tile(w_slot, (K, 1)).astype(np.float32),
        "offs": striped(slot_token),
        "pos1": striped(pos[0]),
        "pos2": striped(pos[1]),
    }


def reference(xT, w1, w3, w2, gate, offs, pos1, pos2):
    idx = unstriped(offs)
    xq = mxq(f64(gate) * f64(xT)[:, idx], 0, "e4m3")
    h = gelu(by_expert(mxq(f64(w1), 1, "e4m3"), xq))
    h = h * by_expert(mxq(f64(w3), 1, "e4m3"), xq)
    y = by_expert(mxq(f64(w2), 1, "e4m3"), mxq(h, 0, "e4m3"))
    return y[:, unstriped(pos1)] + y[:, unstriped(pos2)]

@@ -1,0 +1,247 @@
+from contextlib import ExitStack
+
+import concourse.mybir as mybir
+from concourse.masks import make_identity
+
+K, T, E, C, H, N = 512, 1280, 10, 256, 512, 128
+S = E * C
+FLOPS = 2 * S * (2 * K * H + H * N)
+BYTES = 4 * (K * T + 2 * E * K * H + E * H * N + S + N * T) + 2 * 128 * (S + 2 * T) // 16
+
+F32 = mybir.dt.float32
+BF16 = mybir.dt.bfloat16
+U32 = mybir.dt.uint32
+U16 = mybir.dt.uint16
+U8 = mybir.dt.uint8
+FP8X4 = mybir.dt.float8_e4m3fn_x4
+MULT = mybir.AluOpType.mult
+ADD = mybir.AluOpType.add
+GELU = mybir.ActivationFunctionType.Gelu_apprx_tanh
+
+P = 128
+PACK = 4
+HALF = 128
+BANK = 512
+GROUPS = (512, 512, 512, 512, 512)
+HEAD = "x0 a0 x1 b0 a1 x2 b1 a2 x3 c0 b2 c1"
+RAW_BUFS = 6
+XC_BUFS = 3
+XB_BUFS = 3
+WC_BUFS = 8
+ACT_BUFS = 3
+HB_BUFS = 3
+GATHER_AHEAD = 1
+XG_BUFS = 3
+WB_BUFS = 4
+X_ON_SCALAR = ()
+W2_ON_SCALAR = (0, 1, 2, 3, 4, 5)
+Y_ON_VECTOR = ()
+LAG1 = 1
+LAG2 = 2
+OUT_PIECES = (512, 448, 320)
+W3_ON_VECTOR = (7, 8, 9)
+
+
+def tile_moe_pre_glu_gelu_kernel(
+    tc, xT, w1, w3, w2, gate, offs, pos1, pos2, out
+):
+    nc = tc.nc
+
+    def copy_on(engine, dst, src):
+        if engine == "vector":
+            nc.vector.tensor_copy(out=dst, in_=src)
+        else:
+            nc.scalar.copy(out=dst, in_=src)
+
+    def interleave(engine, dst, src):
+        copy_on(
+            engine,
+            dst.rearrange("p (c i j) -> p c j i", i=4, j=PACK),
+            src.rearrange("p j (c i) -> p c j i", i=4),
+        )
+
+    def interleave_permuted(engine, dst, src):
+        copy_on(
+            engine,
+            dst.rearrange("p (t m j) -> p m j t", t=PACK, j=PACK),
+            src.rearrange("p j (m t) -> p m j t", t=PACK),
+        )
+
+    def quantize(codes, scales, values):
+        nc.vector.quantize_mx(out=codes.bitcast(FP8X4), scales=scales, in_=values)
+
+    def product(acc, w_codes, w_scales, x_codes, x_scales):
+        nc.tensor.matmul_mx(
+            out=acc,
+            lhsT=w_codes.bitcast(FP8X4),
+            lhsT_scale=w_scales,
+            rhs=x_codes.bitcast(FP8X4),
+            rhs_scale=x_scales,
+            start=True,
+            stop=True,
+        )
+
+    with ExitStack() as ctx:
+        keep = ctx.enter_context(tc.tile_pool(name="keep", bufs=1))
+        raw = ctx.enter_context(tc.tile_pool(name="raw", bufs=7))
+        work = ctx.enter_context(tc.tile_pool(name="work", bufs=3))
+        psum = ctx.enter_context(tc.psum_pool(name="psum", bufs=3))
+        psum_y = ctx.enter_context(tc.psum_pool(name="psum_y", bufs=2))
+
+        offs_sb = keep.tile([P, S // 16], U16, name="offs_sb")
+        pos1_sb = keep.tile([P, T // 16], U16, name="pos1_sb")
+        pos2_sb = keep.tile([P, T // 16], U16, name="pos2_sb")
+        x_rows = [keep.tile([P, T], F32, name="x_row%d" % j) for j in range(PACK)]
+        y_all = keep.tile([P, S], F32, name="y_all")
+        warm = keep.tile([P, 2], F32, name="warm")
+
+        nc.vector.memset(warm[:, 0:1], 0.0)
+        nc.scalar.activation(out=warm[:, 1:2], in_=warm[:, 0:1], func=GELU)
+
+        x_view = xT.rearrange("(p j) t -> p j t", j=PACK)
+        starts = [sum(GROUPS[:g]) for g in range(len(GROUPS))]
+        gates = [keep.tile([P, BANK], F32, name="gate%d" % g) for g in range(S // BANK)]
+        gate_cols = keep.tile([P, S // BANK, PACK], F32, name="gate_cols", tag="first", align_bytes=64)
+        identity = keep.tile([P, P], F32, name="identity")
+        make_identity(nc, identity[:])
+        nc.sync.dma_start(gate_cols[:], gate[0].rearrange("(g n i) -> n g i", n=P, i=PACK))
+        for g in range(S // BANK):
+            spread = psum.tile([P, PACK, P], F32, name="spread", tag="a_ps" if g % 2 == 0 else "b_ps")
+            for i in range(PACK):
+                nc.tensor.transpose(spread[:, i, :], gate_cols[:, g, i : i + 1].to_broadcast([P, P]), identity[:])
+            nc.scalar.copy(
+                out=gates[g][:].rearrange("p (n i) -> p n i", i=PACK),
+                in_=spread[:].rearrange("p i n -> p n i"),
+            )
+
+        def load_weights(w, e, width, tag, bufs):
+            t = raw.tile([P, PACK, width], F32, name=tag, tag=tag, bufs=bufs)
+            nc.sync.dma_start(t[:], w[e].rearrange("(p j) c -> p j c", j=PACK))
+            return t
+
+        loaded = {}
+
+        def load(kind, i):
+            if (kind, i) in loaded:
+                return loaded[kind, i]
+            if kind == "x":
+                nc.sync.dma_start(x_rows[i][:], x_view[:, i, :])
+                loaded[kind, i] = x_rows[i]
+            elif kind == "a":
+                loaded[kind, i] = load_weights(w1, i, H, "w_raw", RAW_BUFS)
+            elif kind == "b":
+                loaded[kind, i] = load_weights(w3, i, H, "w_raw", RAW_BUFS)
+            else:
+                loaded[kind, i] = load_weights(w2, i, N, "w2_raw", 4)
+            return loaded[kind, i]
+
+        nc.sync.dma_start(offs_sb[:], offs)
+        for item in HEAD.split():
+            load(item[0], int(item[1:]))
+
+        x_codes = {}
+
+        def gather_group(g):
+            s0, n = starts[g], GROUPS[g]
+            xg = work.tile([P, PACK, n], F32, name="xg", tag="xg", bufs=XG_BUFS)
+            for j in range(PACK):
+                nc.vector.tensor_tensor(
+                    out=xg[:, j, :],
+                    in0=x_rows[j][:].indirect(offs_sb[:, s0 // 16 : (s0 + n) // 16]),
+                    in1=gates[s0 // BANK][:, s0 % BANK : s0 % BANK + n],
+                    op=MULT,
+                )
+            return xg
+
+        gathered = {}
+
+        def quantize_tokens(e):
+            g = max(i for i in range(len(GROUPS)) if starts[i] <= e * C)
+            c0 = e * C - starts[g]
+            xb = work.tile([P, C * PACK], BF16, name="xb", tag="xb", bufs=XB_BUFS, align_bytes=64)
+            interleave("scalar" if e in X_ON_SCALAR else "vector", xb[:], gathered[g][:, :, c0 : c0 + C])
+            xc = work.tile([P, C], U32, name="xc", tag="xc", bufs=XC_BUFS, align_bytes=64)
+            xs = work.tile([P, C], U8, name="xs", tag="xs", bufs=XC_BUFS, align_bytes=64)
+            quantize(xc[:], xs[:], xb[:])
+            return xc, xs
+
+        def quantize_first(w_raw, engine, first=False):
+            if first:
+                wb = keep.tile([P, H * PACK], BF16, name="wb0", tag="first", align_bytes=64)
+            else:
+                wb = work.tile([P, H * PACK], BF16, name="wb", tag="wb", bufs=WB_BUFS, align_bytes=64)
+            interleave_permuted(engine, wb[:], w_raw[:])
+            wc = work.tile([P, H], U32, name="wc", tag="wc", bufs=WC_BUFS, align_bytes=64)
+            ws = work.tile([P, H], U8, name="ws", tag="ws", bufs=WC_BUFS, align_bytes=64)
+            quantize(wc[:], ws[:], wb[:])
+            return wc, ws
+
+        def prepare(e):
+            for g in range(len(GROUPS)):
+                if g not in gathered and starts[g] <= (e + GATHER_AHEAD) * C:
+                    gathered[g] = gather_group(g)
+            x_q = quantize_tokens(e)
+            w1_raw = load("a", e)
+            w3_raw = load("b", e)
+            w2_raw = load("c", e)
+            if e == E // 2:
+                nc.sync.dma_start(pos1_sb[:], pos1)
+                nc.sync.dma_start(pos2_sb[:], pos2)
+            w1_q = quantize_first(w1_raw, "scalar", e == 0)
+            w3_q = quantize_first(w3_raw, "vector" if e in W3_ON_VECTOR else "scalar")
+            w2b = work.tile([P, N * PACK], BF16, name="w2b", tag="w2b", align_bytes=64)
+            interleave("scalar" if e in W2_ON_SCALAR else "vector", w2b[:], w2_raw[:])
+            w2c = work.tile([P, N], U32, name="w2c", tag="w2c", align_bytes=64)
+            w2s = work.tile([P, N], U8, name="w2s", tag="w2s", align_bytes=64)
+            quantize(w2c[:], w2s[:], w2b[:])
+            return x_q, w1_q, w3_q, (w2c, w2s)
+
+        def first_layer(x_q, w1_q, w3_q):
+            xc, xs = x_q
+            hb = work.tile([P, C, PACK], BF16, name="hb", tag="hb", bufs=HB_BUFS, align_bytes=64)
+            for half in range(C // HALF):
+                cols = slice(half * HALF, (half + 1) * HALF)
+                a_ps = psum.tile([P, PACK, HALF], F32, name="a_ps", tag="a_ps")
+                b_ps = psum.tile([P, PACK, HALF], F32, name="b_ps", tag="b_ps")
+                for acc, (wc, ws) in ((a_ps, w1_q), (b_ps, w3_q)):
+                    for t in range(PACK):
+                        m_cols = slice(t * P, (t + 1) * P)
+                        product(acc[:, t, :], wc[:, m_cols], ws[:, m_cols], xc[:, cols], xs[:, cols])
+                act = work.tile([P, HALF, PACK], F32, name="act", tag="act", bufs=ACT_BUFS)
+                nc.scalar.activation(out=act[:], in_=a_ps[:].rearrange("p t s -> p s t"), func=GELU)
+                nc.vector.tensor_tensor(
+                    out=hb[:, cols, :], in0=b_ps[:].rearrange("p t s -> p s t"), in1=act[:], op=MULT
+                )
+            return hb
+
+        def second_layer(e, hb, w2_q):
+            hc = work.tile([P, C], U32, name="hc", tag="hc", align_bytes=64)
+            hs = work.tile([P, C], U8, name="hs", tag="hs", align_bytes=64)
+            quantize(hc[:], hs[:], hb[:].rearrange("p s t -> p (s t)"))
+            y_ps = psum_y.tile([P, C], F32, name="y_ps", tag="y_ps")
+            product(y_ps[:], w2_q[0][:], w2_q[1][:], hc[:], hs[:])
+            copy_on("vector" if e in Y_ON_VECTOR else "scalar", y_all[:, e * C : (e + 1) * C], y_ps[:])
+
+        ready = {}
+        hidden = {}
+        for step in range(E + LAG2):
+            if step < E:
+                ready[step] = prepare(step)
+            e = step - LAG1
+            if 0 <= e < E:
+                hidden[e] = first_layer(*ready[e][:3])
+            e = step - LAG2
+            if 0 <= e < E:
+                second_layer(e, hidden[e], ready[e][3])
+
+        t0 = 0
+        for i, width in enumerate(OUT_PIECES):
+            lists = slice(t0 // 16, (t0 + width) // 16)
+            first = keep.tile([P, width], F32, name="first%d" % i)
+            total = keep.tile([P, width], F32, name="total%d" % i)
+            nc.vector.tensor_copy(out=first[:], in_=y_all[:].indirect(pos1_sb[:, lists]))
+            nc.vector.tensor_tensor(
+                out=total[:], in0=y_all[:].indirect(pos2_sb[:, lists]), in1=first[:], op=ADD
+            )
+            nc.sync.dma_start(out[:, t0 : t0 + width], total[:])
+            t0 += width

@@ -22,24 +22,37 @@ P = 128
 PACK = 4
 HALF = 128
 BANK = 512
-GROUPS = (512, 512, 512, 512, 512)
-HEAD = "x0 a0 x1 b0 a1 x2 b1 a2 x3 c0 b2 c1"
+RUN = 2
+WPAIR = 0
+XW = 256
+CE = 2
+X_SPLIT = 0
+X_ON_ACT = ()
+PAIRS = 0
+PS_A = 3
+PS_B = 3
+PS_Y = 2
+GROUPS = (256,) * 10
+HEAD = "x0 a0 x1 b0 a1 x2 b1 a2 x3"
 RAW_BUFS = 6
-XC_BUFS = 3
+XC_BUFS = 6
 XB_BUFS = 3
-WC_BUFS = 8
-ACT_BUFS = 3
+WC_BUFS = 4
+ACT_BUFS = 4
 HB_BUFS = 3
-GATHER_AHEAD = 1
-XG_BUFS = 3
+GATHER_AHEAD = 0
+XG_BUFS = 6
 WB_BUFS = 4
-X_ON_SCALAR = ()
-W2_ON_SCALAR = (0, 1, 2, 3, 4, 5)
-Y_ON_VECTOR = ()
+X_ON_SCALAR = (0,)
+W2_ON_SCALAR = tuple(range(10))
+Y_ON_VECTOR = (9,)
 LAG1 = 1
-LAG2 = 2
+LAGW = 2
+C_AHEAD = -9
+C_BUFS = 5
+LAG2 = 3
 OUT_PIECES = (512, 448, 320)
-W3_ON_VECTOR = (7, 8, 9)
+W3_ON_VECTOR = (8, 9)
 
 
 def tile_moe_pre_glu_gelu_kernel(
@@ -56,15 +69,22 @@ def tile_moe_pre_glu_gelu_kernel(
     def interleave(engine, dst, src):
         copy_on(
             engine,
-            dst.rearrange("p (c i j) -> p c j i", i=4, j=PACK),
-            src.rearrange("p j (c i) -> p c j i", i=4),
+            dst.rearrange("p (c i j) -> p c j i", i=RUN, j=PACK),
+            src.rearrange("p j (c i) -> p c j i", i=RUN),
         )
 
     def interleave_permuted(engine, dst, src):
+        if not PAIRS:
+            copy_on(
+                engine,
+                dst.rearrange("p (t m j) -> p m j t", t=PACK, j=PACK),
+                src.rearrange("p j (m t) -> p m j t", t=PACK),
+            )
+            return
         copy_on(
             engine,
-            dst.rearrange("p (t m j) -> p m j t", t=PACK, j=PACK),
-            src.rearrange("p j (m t) -> p m j t", t=PACK),
+            dst.rearrange("p (t c r j) -> p c t j r", t=PACK, r=2, j=PACK),
+            src.rearrange("p j (c t r) -> p c t j r", t=PACK, r=2),
         )
 
     def quantize(codes, scales, values):
@@ -86,7 +106,7 @@ def tile_moe_pre_glu_gelu_kernel(
         raw = ctx.enter_context(tc.tile_pool(name="raw", bufs=7))
         work = ctx.enter_context(tc.tile_pool(name="work", bufs=3))
         psum = ctx.enter_context(tc.psum_pool(name="psum", bufs=3))
-        psum_y = ctx.enter_context(tc.psum_pool(name="psum_y", bufs=2))
+        psum_y = ctx.enter_context(tc.psum_pool(name="psum_y", bufs=PS_Y))
 
         offs_sb = keep.tile([P, S // 16], U16, name="offs_sb")
         pos1_sb = keep.tile([P, T // 16], U16, name="pos1_sb")
@@ -106,7 +126,7 @@ def tile_moe_pre_glu_gelu_kernel(
         make_identity(nc, identity[:])
         nc.sync.dma_start(gate_cols[:], gate[0].rearrange("(g n i) -> n g i", n=P, i=PACK))
         for g in range(S // BANK):
-            spread = psum.tile([P, PACK, P], F32, name="spread", tag="a_ps" if g % 2 == 0 else "b_ps")
+            spread = psum.tile([P, PACK, P], F32, name="spread", tag="a_ps" if g % 2 == 0 else "b_ps", bufs=PS_A if g % 2 == 0 else PS_B)
             for i in range(PACK):
                 nc.tensor.transpose(spread[:, i, :], gate_cols[:, g, i : i + 1].to_broadcast([P, P]), identity[:])
             nc.scalar.copy(
@@ -125,14 +145,31 @@ def tile_moe_pre_glu_gelu_kernel(
             if (kind, i) in loaded:
                 return loaded[kind, i]
             if kind == "x":
-                nc.sync.dma_start(x_rows[i][:], x_view[:, i, :])
+                if X_SPLIT and i == 0:
+                    nc.sync.dma_start(x_rows[i][:, 0 : T // 2], x_view[:, i, 0 : T // 2])
+                    nc.scalar.dma_start(x_rows[i][:, T // 2 : T], x_view[:, i, T // 2 : T])
+                elif i in X_ON_ACT:
+                    nc.scalar.dma_start(x_rows[i][:], x_view[:, i, :])
+                else:
+                    nc.sync.dma_start(x_rows[i][:], x_view[:, i, :])
                 loaded[kind, i] = x_rows[i]
             elif kind == "a":
                 loaded[kind, i] = load_weights(w1, i, H, "w_raw", RAW_BUFS)
             elif kind == "b":
                 loaded[kind, i] = load_weights(w3, i, H, "w_raw", RAW_BUFS)
             else:
-                loaded[kind, i] = load_weights(w2, i, N, "w2_raw", 4)
+                t = raw.tile([P, CE, PACK, N], F32, name="w2_raw", tag="w2_raw", bufs=C_BUFS)
+                if PAIRS:
+                    rows = w2[i].rearrange("(c t r) n -> r c t n", t=PACK, r=2)
+                    for r in range(2):
+                        nc.sync.dma_start(t[r:P:2, 0, :, :], rows[r])
+                else:
+                    nc.sync.dma_start(
+                        t[:].rearrange("p e j n -> p e (j n)"),
+                        w2[i : i + CE].rearrange("e (p j) n -> p e (j n)", j=PACK),
+                    )
+                for k in range(CE):
+                    loaded[kind, i + k] = t
             return loaded[kind, i]
 
         nc.sync.dma_start(offs_sb[:], offs)
@@ -155,15 +192,22 @@ def tile_moe_pre_glu_gelu_kernel(
 
         gathered = {}
 
+        tokens_q = {}
+
         def quantize_tokens(e):
+            if e in tokens_q:
+                return tokens_q[e]
             g = max(i for i in range(len(GROUPS)) if starts[i] <= e * C)
             c0 = e * C - starts[g]
-            xb = work.tile([P, C * PACK], BF16, name="xb", tag="xb", bufs=XB_BUFS, align_bytes=64)
-            interleave("scalar" if e in X_ON_SCALAR else "vector", xb[:], gathered[g][:, :, c0 : c0 + C])
-            xc = work.tile([P, C], U32, name="xc", tag="xc", bufs=XC_BUFS, align_bytes=64)
-            xs = work.tile([P, C], U8, name="xs", tag="xs", bufs=XC_BUFS, align_bytes=64)
+            n = min(XW, GROUPS[g] - c0)
+            xb = work.tile([P, n * PACK], BF16, name="xb", tag="xb", bufs=XB_BUFS, align_bytes=64)
+            interleave("scalar" if e in X_ON_SCALAR else "vector", xb[:], gathered[g][:, :, c0 : c0 + n])
+            xc = work.tile([P, n], U32, name="xc", tag="xc", bufs=XC_BUFS, align_bytes=64)
+            xs = work.tile([P, n], U8, name="xs", tag="xs", bufs=XC_BUFS, align_bytes=64)
             quantize(xc[:], xs[:], xb[:])
-            return xc, xs
+            for i in range(n // C):
+                tokens_q[e + i] = (xc[:, i * C : (i + 1) * C], xs[:, i * C : (i + 1) * C])
+            return tokens_q[e]
 
         def quantize_first(w_raw, engine, first=False):
             if first:
@@ -176,6 +220,18 @@ def tile_moe_pre_glu_gelu_kernel(
             quantize(wc[:], ws[:], wb[:])
             return wc, ws
 
+        def quantize_both(w1_raw, w3_raw, engine, first):
+            if first:
+                wb = keep.tile([P, 2, H * PACK], BF16, name="wb0", tag="first", align_bytes=64)
+            else:
+                wb = work.tile([P, 2, H * PACK], BF16, name="wb", tag="wb", bufs=(WB_BUFS + 1) // 2, align_bytes=64)
+            interleave_permuted("scalar", wb[:, 0, :], w1_raw[:])
+            interleave_permuted(engine, wb[:, 1, :], w3_raw[:])
+            wc = work.tile([P, 2 * H], U32, name="wc", tag="wc", bufs=WC_BUFS // 2, align_bytes=64)
+            ws = work.tile([P, 2 * H], U8, name="ws", tag="ws", bufs=WC_BUFS // 2, align_bytes=64)
+            quantize(wc[:], ws[:], wb[:].rearrange("p a b -> p (a b)"))
+            return (wc[:, 0:H], ws[:, 0:H]), (wc[:, H : 2 * H], ws[:, H : 2 * H])
+
         def prepare(e):
             for g in range(len(GROUPS)):
                 if g not in gathered and starts[g] <= (e + GATHER_AHEAD) * C:
@@ -183,26 +239,42 @@ def tile_moe_pre_glu_gelu_kernel(
             x_q = quantize_tokens(e)
             w1_raw = load("a", e)
             w3_raw = load("b", e)
-            w2_raw = load("c", e)
+            if 0 <= e + C_AHEAD < E and (e + C_AHEAD) % CE == 0:
+                load("c", e + C_AHEAD)
             if e == E // 2:
                 nc.sync.dma_start(pos1_sb[:], pos1)
                 nc.sync.dma_start(pos2_sb[:], pos2)
+            if WPAIR:
+                w1_q, w3_q = quantize_both(w1_raw, w3_raw, "vector" if e in W3_ON_VECTOR else "scalar", e == 0)
+                return x_q, w1_q, w3_q
             w1_q = quantize_first(w1_raw, "scalar", e == 0)
             w3_q = quantize_first(w3_raw, "vector" if e in W3_ON_VECTOR else "scalar")
-            w2b = work.tile([P, N * PACK], BF16, name="w2b", tag="w2b", align_bytes=64)
-            interleave("scalar" if e in W2_ON_SCALAR else "vector", w2b[:], w2_raw[:])
-            w2c = work.tile([P, N], U32, name="w2c", tag="w2c", align_bytes=64)
-            w2s = work.tile([P, N], U8, name="w2s", tag="w2s", align_bytes=64)
+            return x_q, w1_q, w3_q
+
+        def prepare_second(e):
+            if e in second:
+                return second[e]
+            w2_raw = load("c", e)
+            w2b = work.tile([P, CE * N * PACK], BF16, name="w2b", tag="w2b", align_bytes=64)
+            copy_on(
+                "scalar" if e in W2_ON_SCALAR else "vector",
+                w2b[:].rearrange("p (e c i j) -> p e c j i", e=CE, i=RUN, j=PACK),
+                w2_raw[:].rearrange("p e j (c i) -> p e c j i", i=RUN),
+            )
+            w2c = work.tile([P, CE * N], U32, name="w2c", tag="w2c", align_bytes=64)
+            w2s = work.tile([P, CE * N], U8, name="w2s", tag="w2s", align_bytes=64)
             quantize(w2c[:], w2s[:], w2b[:])
-            return x_q, w1_q, w3_q, (w2c, w2s)
+            for k in range(CE):
+                second[e + k] = (w2c[:, k * N : (k + 1) * N], w2s[:, k * N : (k + 1) * N])
+            return second[e]
 
         def first_layer(x_q, w1_q, w3_q):
             xc, xs = x_q
             hb = work.tile([P, C, PACK], BF16, name="hb", tag="hb", bufs=HB_BUFS, align_bytes=64)
             for half in range(C // HALF):
                 cols = slice(half * HALF, (half + 1) * HALF)
-                a_ps = psum.tile([P, PACK, HALF], F32, name="a_ps", tag="a_ps")
-                b_ps = psum.tile([P, PACK, HALF], F32, name="b_ps", tag="b_ps")
+                a_ps = psum.tile([P, PACK, HALF], F32, name="a_ps", tag="a_ps", bufs=PS_A)
+                b_ps = psum.tile([P, PACK, HALF], F32, name="b_ps", tag="b_ps", bufs=PS_B)
                 for acc, (wc, ws) in ((a_ps, w1_q), (b_ps, w3_q)):
                     for t in range(PACK):
                         m_cols = slice(t * P, (t + 1) * P)
@@ -219,20 +291,24 @@ def tile_moe_pre_glu_gelu_kernel(
             hs = work.tile([P, C], U8, name="hs", tag="hs", align_bytes=64)
             quantize(hc[:], hs[:], hb[:].rearrange("p s t -> p (s t)"))
             y_ps = psum_y.tile([P, C], F32, name="y_ps", tag="y_ps")
-            product(y_ps[:], w2_q[0][:], w2_q[1][:], hc[:], hs[:])
+            product(y_ps[:], w2_q[0], w2_q[1], hc[:], hs[:])
             copy_on("vector" if e in Y_ON_VECTOR else "scalar", y_all[:, e * C : (e + 1) * C], y_ps[:])
 
         ready = {}
         hidden = {}
+        second = {}
         for step in range(E + LAG2):
             if step < E:
                 ready[step] = prepare(step)
+            e = step - LAGW
+            if 0 <= e < E:
+                second[e] = prepare_second(e)
             e = step - LAG1
             if 0 <= e < E:
-                hidden[e] = first_layer(*ready[e][:3])
+                hidden[e] = first_layer(*ready[e])
             e = step - LAG2
             if 0 <= e < E:
-                second_layer(e, hidden[e], ready[e][3])
+                second_layer(e, hidden[e], second[e])
 
         t0 = 0
         for i, width in enumerate(OUT_PIECES):

@@ -32,16 +32,16 @@ PAIRS = 0
 PS_A = 3
 PS_B = 3
 PS_Y = 2
-GROUPS = (256,) * 10
+GROUPS = (256, 256, 512, 512, 512, 512)
 HEAD = "x0 a0 x1 b0 a1 x2 b1 a2 x3"
-RAW_BUFS = 6
+RAW_BUFS = 7
 XC_BUFS = 6
-XB_BUFS = 3
-WC_BUFS = 4
+XB_BUFS = 2
+WC_BUFS = 6
 ACT_BUFS = 4
 HB_BUFS = 3
 GATHER_AHEAD = 0
-XG_BUFS = 6
+XG_BUFS = 4
 WB_BUFS = 4
 X_ON_SCALAR = (0,)
 W2_ON_SCALAR = tuple(range(10))
@@ -49,9 +49,10 @@ Y_ON_VECTOR = (9,)
 LAG1 = 1
 LAGW = 2
 C_AHEAD = -9
-C_BUFS = 5
+C_BUFS = 3
 LAG2 = 3
-OUT_PIECES = (512, 448, 320)
+OUT_PIECES = (640, 512, 128)
+FIRST_PIECES = (640, 640)
 W3_ON_VECTOR = (8, 9)
 
 
@@ -120,7 +121,7 @@ def tile_moe_pre_glu_gelu_kernel(
 
         x_view = xT.rearrange("(p j) t -> p j t", j=PACK)
         starts = [sum(GROUPS[:g]) for g in range(len(GROUPS))]
-        gates = [keep.tile([P, BANK], F32, name="gate%d" % g) for g in range(S // BANK)]
+        gate_all = keep.tile([P, S], F32, name="gate_all")
         gate_cols = keep.tile([P, S // BANK, PACK], F32, name="gate_cols", tag="first", align_bytes=64)
         identity = keep.tile([P, P], F32, name="identity")
         make_identity(nc, identity[:])
@@ -130,7 +131,7 @@ def tile_moe_pre_glu_gelu_kernel(
             for i in range(PACK):
                 nc.tensor.transpose(spread[:, i, :], gate_cols[:, g, i : i + 1].to_broadcast([P, P]), identity[:])
             nc.scalar.copy(
-                out=gates[g][:].rearrange("p (n i) -> p n i", i=PACK),
+                out=gate_all[:, g * BANK : (g + 1) * BANK].rearrange("p (n i) -> p n i", i=PACK),
                 in_=spread[:].rearrange("p i n -> p n i"),
             )
 
@@ -185,7 +186,7 @@ def tile_moe_pre_glu_gelu_kernel(
                 nc.vector.tensor_tensor(
                     out=xg[:, j, :],
                     in0=x_rows[j][:].indirect(offs_sb[:, s0 // 16 : (s0 + n) // 16]),
-                    in1=gates[s0 // BANK][:, s0 % BANK : s0 % BANK + n],
+                    in1=gate_all[:, s0 : s0 + n],
                     op=MULT,
                 )
             return xg
@@ -279,10 +280,13 @@ def tile_moe_pre_glu_gelu_kernel(
                     for t in range(PACK):
                         m_cols = slice(t * P, (t + 1) * P)
                         product(acc[:, t, :], wc[:, m_cols], ws[:, m_cols], xc[:, cols], xs[:, cols])
-                act = work.tile([P, HALF, PACK], F32, name="act", tag="act", bufs=ACT_BUFS)
-                nc.scalar.activation(out=act[:], in_=a_ps[:].rearrange("p t s -> p s t"), func=GELU)
+                act = work.tile([P, HALF // 2, PACK, 2], F32, name="act", tag="act", bufs=ACT_BUFS)
+                nc.scalar.activation(out=act[:], in_=a_ps[:].rearrange("p t (c i) -> p c t i", i=2), func=GELU)
                 nc.vector.tensor_tensor(
-                    out=hb[:, cols, :], in0=b_ps[:].rearrange("p t s -> p s t"), in1=act[:], op=MULT
+                    out=hb[:, cols, :].rearrange("p (c i) t -> p c t i", i=2),
+                    in0=b_ps[:].rearrange("p t (c i) -> p c t i", i=2),
+                    in1=act[:],
+                    op=MULT,
                 )
             return hb
 
@@ -310,14 +314,21 @@ def tile_moe_pre_glu_gelu_kernel(
             if 0 <= e < E:
                 second_layer(e, hidden[e], second[e])
 
+        first = keep.tile([P, T], F32, name="first_results")
+        t0 = 0
+        for width in FIRST_PIECES:
+            nc.vector.tensor_copy(
+                out=first[:, t0 : t0 + width], in_=y_all[:].indirect(pos1_sb[:, t0 // 16 : (t0 + width) // 16])
+            )
+            t0 += width
         t0 = 0
         for i, width in enumerate(OUT_PIECES):
-            lists = slice(t0 // 16, (t0 + width) // 16)
-            first = keep.tile([P, width], F32, name="first%d" % i)
             total = keep.tile([P, width], F32, name="total%d" % i)
-            nc.vector.tensor_copy(out=first[:], in_=y_all[:].indirect(pos1_sb[:, lists]))
             nc.vector.tensor_tensor(
-                out=total[:], in0=y_all[:].indirect(pos2_sb[:, lists]), in1=first[:], op=ADD
+                out=total[:],
+                in0=y_all[:].indirect(pos2_sb[:, t0 // 16 : (t0 + width) // 16]),
+                in1=first[:, t0 : t0 + width],
+                op=ADD,
             )
             nc.sync.dma_start(out[:, t0 : t0 + width], total[:])
             t0 += width

@@ -23,6 +23,8 @@ PACK = 4
 HALF = 128
 BANK = 512
 RUN = 2
+YPAIR = 8
+HC_BUFS = 2
 WPAIR = 0
 XW = 256
 CE = 2
@@ -36,21 +38,21 @@ GROUPS = (256, 256, 512, 512, 512, 512)
 HEAD = "x0 a0 x1 b0 a1 x2 b1 a2 x3"
 RAW_BUFS = 7
 XC_BUFS = 6
-XB_BUFS = 2
-WC_BUFS = 6
+XB_BUFS = 3
+WC_BUFS = 4
 ACT_BUFS = 4
-HB_BUFS = 3
+HB_BUFS = 2
 GATHER_AHEAD = 0
 XG_BUFS = 4
 WB_BUFS = 4
-X_ON_SCALAR = (0,)
-W2_ON_SCALAR = tuple(range(10))
+X_ON_SCALAR = ()
+W2_ON_SCALAR = tuple(range(2, 10))
 Y_ON_VECTOR = (9,)
-LAG1 = 1
-LAGW = 2
+LAG1 = 2
+LAGW = 3
 C_AHEAD = -9
 C_BUFS = 3
-LAG2 = 3
+LAG2 = 4
 OUT_PIECES = (640, 512, 128)
 FIRST_PIECES = (640, 640)
 W3_ON_VECTOR = (8, 9)
@@ -70,16 +72,16 @@ def tile_moe_pre_glu_gelu_kernel(
     def interleave(engine, dst, src):
         copy_on(
             engine,
-            dst.rearrange("p (c i j) -> p c j i", i=RUN, j=PACK),
-            src.rearrange("p j (c i) -> p c j i", i=RUN),
+            dst.rearrange("p (c i u v) -> p c u i v", i=4, u=2, v=2),
+            src.rearrange("p (u v) (c i) -> p c u i v", i=4, v=2),
         )
 
     def interleave_permuted(engine, dst, src):
         if not PAIRS:
             copy_on(
                 engine,
-                dst.rearrange("p (t m j) -> p m j t", t=PACK, j=PACK),
-                src.rearrange("p j (m t) -> p m j t", t=PACK),
+                dst.rearrange("p (t m u v) -> p m u t v", t=PACK, u=2, v=2),
+                src.rearrange("p (u v) (m t) -> p m u t v", t=PACK, v=2),
             )
             return
         copy_on(
@@ -257,11 +259,12 @@ def tile_moe_pre_glu_gelu_kernel(
                 return second[e]
             w2_raw = load("c", e)
             w2b = work.tile([P, CE * N * PACK], BF16, name="w2b", tag="w2b", align_bytes=64)
-            copy_on(
-                "scalar" if e in W2_ON_SCALAR else "vector",
-                w2b[:].rearrange("p (e c i j) -> p e c j i", e=CE, i=RUN, j=PACK),
-                w2_raw[:].rearrange("p e j (c i) -> p e c j i", i=RUN),
-            )
+            for k in range(CE):
+                interleave(
+                    "scalar" if e in W2_ON_SCALAR else "vector",
+                    w2b[:, k * N * PACK : (k + 1) * N * PACK],
+                    w2_raw[:, k, :, :],
+                )
             w2c = work.tile([P, CE * N], U32, name="w2c", tag="w2c", align_bytes=64)
             w2s = work.tile([P, CE * N], U8, name="w2s", tag="w2s", align_bytes=64)
             quantize(w2c[:], w2s[:], w2b[:])
@@ -280,24 +283,30 @@ def tile_moe_pre_glu_gelu_kernel(
                     for t in range(PACK):
                         m_cols = slice(t * P, (t + 1) * P)
                         product(acc[:, t, :], wc[:, m_cols], ws[:, m_cols], xc[:, cols], xs[:, cols])
-                act = work.tile([P, HALF // 2, PACK, 2], F32, name="act", tag="act", bufs=ACT_BUFS)
-                nc.scalar.activation(out=act[:], in_=a_ps[:].rearrange("p t (c i) -> p c t i", i=2), func=GELU)
+                act = work.tile([P, HALF, PACK], F32, name="act", tag="act", bufs=ACT_BUFS)
+                nc.scalar.activation(out=act[:], in_=a_ps[:].rearrange("p t s -> p s t"), func=GELU)
                 nc.vector.tensor_tensor(
-                    out=hb[:, cols, :].rearrange("p (c i) t -> p c t i", i=2),
-                    in0=b_ps[:].rearrange("p t (c i) -> p c t i", i=2),
-                    in1=act[:],
-                    op=MULT,
+                    out=hb[:, cols, :], in0=b_ps[:].rearrange("p t s -> p s t"), in1=act[:], op=MULT
                 )
             return hb
 
         def second_layer(e, hb, w2_q):
-            hc = work.tile([P, C], U32, name="hc", tag="hc", align_bytes=64)
-            hs = work.tile([P, C], U8, name="hs", tag="hs", align_bytes=64)
+            hc = work.tile([P, C], U32, name="hc", tag="hc", bufs=HC_BUFS, align_bytes=64)
+            hs = work.tile([P, C], U8, name="hs", tag="hs", bufs=HC_BUFS, align_bytes=64)
             quantize(hc[:], hs[:], hb[:].rearrange("p s t -> p (s t)"))
+            if YPAIR and e < YPAIR:
+                if e % 2 == 0:
+                    y_banks[e // 2] = psum_y.tile([P, 2 * C], F32, name="y_ps", tag="y_ps")
+                y_ps = y_banks[e // 2]
+                product(y_ps[:, (e % 2) * C : (e % 2 + 1) * C], w2_q[0], w2_q[1], hc[:], hs[:])
+                if e % 2 == 1:
+                    copy_on("vector" if e in Y_ON_VECTOR else "scalar", y_all[:, (e - 1) * C : (e + 1) * C], y_ps[:])
+                return
             y_ps = psum_y.tile([P, C], F32, name="y_ps", tag="y_ps")
             product(y_ps[:], w2_q[0], w2_q[1], hc[:], hs[:])
             copy_on("vector" if e in Y_ON_VECTOR else "scalar", y_all[:, e * C : (e + 1) * C], y_ps[:])
 
+        y_banks = {}
         ready = {}
         hidden = {}
         second = {}

@@ -20,42 +20,16 @@ GELU = mybir.ActivationFunctionType.Gelu_apprx_tanh
 
 P = 128
 PACK = 4
-HALF = 128
+LIST = 16
 BANK = 512
-RUN = 2
-YPAIR = 8
-HC_BUFS = 2
-WPAIR = 0
-XW = 256
-CE = 2
-X_SPLIT = 0
-X_ON_ACT = ()
-PAIRS = 0
-PS_A = 3
-PS_B = 3
-PS_Y = 2
-GROUPS = (256, 256, 512, 512, 512, 512)
-HEAD = "x0 a0 x1 b0 a1 x2 b1 a2 x3"
-RAW_BUFS = 7
-XC_BUFS = 6
-XB_BUFS = 3
-WC_BUFS = 4
-ACT_BUFS = 4
-HB_BUFS = 2
-GATHER_AHEAD = 0
-XG_BUFS = 4
-WB_BUFS = 4
-X_ON_SCALAR = ()
-W2_ON_SCALAR = tuple(range(2, 10))
-Y_ON_VECTOR = (9,)
-LAG1 = 2
-LAGW = 3
-C_AHEAD = -9
-C_BUFS = 3
-LAG2 = 4
-OUT_PIECES = (640, 512, 128)
-FIRST_PIECES = (640, 640)
-W3_ON_VECTOR = (8, 9)
+HALF = BANK // PACK
+PAIR = 2
+
+GATHERS = (C, C) + (PAIR * C,) * ((E - 2) // PAIR)
+W3_ON_VECTOR_FROM = E - 2
+W2_ON_SCALAR_FROM = PAIR
+FIRST_LAYER_LAG, W2_LAG, SECOND_LAYER_LAG = 2, 3, 4
+STORE_WIDTHS = (640, 512, 128)
 
 
 def tile_moe_pre_glu_gelu_kernel(
@@ -63,73 +37,69 @@ def tile_moe_pre_glu_gelu_kernel(
 ):
     nc = tc.nc
 
-    def copy_on(engine, dst, src):
-        if engine == "vector":
+    def copy_on(on_vector, dst, src):
+        if on_vector:
             nc.vector.tensor_copy(out=dst, in_=src)
         else:
             nc.scalar.copy(out=dst, in_=src)
 
-    def interleave(engine, dst, src):
+    def round_rows(on_vector, dst, src):
         copy_on(
-            engine,
+            on_vector,
             dst.rearrange("p (c i u v) -> p c u i v", i=4, u=2, v=2),
             src.rearrange("p (u v) (c i) -> p c u i v", i=4, v=2),
         )
 
-    def interleave_permuted(engine, dst, src):
-        if not PAIRS:
-            copy_on(
-                engine,
-                dst.rearrange("p (t m u v) -> p m u t v", t=PACK, u=2, v=2),
-                src.rearrange("p (u v) (m t) -> p m u t v", t=PACK, v=2),
-            )
-            return
+    def round_rows_permuted(on_vector, dst, src):
         copy_on(
-            engine,
-            dst.rearrange("p (t c r j) -> p c t j r", t=PACK, r=2, j=PACK),
-            src.rearrange("p j (c t r) -> p c t j r", t=PACK, r=2),
+            on_vector,
+            dst.rearrange("p (t m u v) -> p m u t v", t=PACK, u=2, v=2),
+            src.rearrange("p (u v) (m t) -> p m u t v", t=PACK, v=2),
         )
 
-    def quantize(codes, scales, values):
-        nc.vector.quantize_mx(out=codes.bitcast(FP8X4), scales=scales, in_=values)
-
-    def product(acc, w_codes, w_scales, x_codes, x_scales):
+    def product(acc, stationary, moving):
         nc.tensor.matmul_mx(
             out=acc,
-            lhsT=w_codes.bitcast(FP8X4),
-            lhsT_scale=w_scales,
-            rhs=x_codes.bitcast(FP8X4),
-            rhs_scale=x_scales,
+            lhsT=stationary[0].bitcast(FP8X4),
+            lhsT_scale=stationary[1],
+            rhs=moving[0].bitcast(FP8X4),
+            rhs_scale=moving[1],
             start=True,
             stop=True,
         )
+
+    def columns(operand, start, width):
+        return operand[0][:, start : start + width], operand[1][:, start : start + width]
+
+    def entries(list_sb, start, count):
+        return list_sb[:, start // LIST : (start + count) // LIST]
 
     with ExitStack() as ctx:
         keep = ctx.enter_context(tc.tile_pool(name="keep", bufs=1))
         raw = ctx.enter_context(tc.tile_pool(name="raw", bufs=7))
         work = ctx.enter_context(tc.tile_pool(name="work", bufs=3))
         psum = ctx.enter_context(tc.psum_pool(name="psum", bufs=3))
-        psum_y = ctx.enter_context(tc.psum_pool(name="psum_y", bufs=PS_Y))
+        psum_y = ctx.enter_context(tc.psum_pool(name="psum_y", bufs=2))
 
-        offs_sb = keep.tile([P, S // 16], U16, name="offs_sb")
-        pos1_sb = keep.tile([P, T // 16], U16, name="pos1_sb")
-        pos2_sb = keep.tile([P, T // 16], U16, name="pos2_sb")
+        def quantize(values, width, tag, bufs):
+            codes = work.tile([P, width], U32, name=tag + "c", tag=tag + "c", bufs=bufs, align_bytes=64)
+            scales = work.tile([P, width], U8, name=tag + "s", tag=tag + "s", bufs=bufs, align_bytes=64)
+            nc.vector.quantize_mx(out=codes[:].bitcast(FP8X4), scales=scales[:], in_=values)
+            return codes, scales
+
+        offs_sb = keep.tile([P, S // LIST], U16, name="offs_sb")
+        pos1_sb = keep.tile([P, T // LIST], U16, name="pos1_sb")
+        pos2_sb = keep.tile([P, T // LIST], U16, name="pos2_sb")
         x_rows = [keep.tile([P, T], F32, name="x_row%d" % j) for j in range(PACK)]
         y_all = keep.tile([P, S], F32, name="y_all")
-        warm = keep.tile([P, 2], F32, name="warm")
 
-        nc.vector.memset(warm[:, 0:1], 0.0)
-        nc.scalar.activation(out=warm[:, 1:2], in_=warm[:, 0:1], func=GELU)
-
-        x_view = xT.rearrange("(p j) t -> p j t", j=PACK)
-        starts = [sum(GROUPS[:g]) for g in range(len(GROUPS))]
         gate_all = keep.tile([P, S], F32, name="gate_all")
         gate_cols = keep.tile([P, S // BANK, PACK], F32, name="gate_cols", tag="first", align_bytes=64)
         identity = keep.tile([P, P], F32, name="identity")
         make_identity(nc, identity[:])
         nc.sync.dma_start(gate_cols[:], gate[0].rearrange("(g n i) -> n g i", n=P, i=PACK))
         for g in range(S // BANK):
-            spread = psum.tile([P, PACK, P], F32, name="spread", tag="a_ps" if g % 2 == 0 else "b_ps", bufs=PS_A if g % 2 == 0 else PS_B)
+            spread = psum.tile([P, PACK, P], F32, name="spread", tag=("a_ps", "b_ps")[g % 2])
             for i in range(PACK):
                 nc.tensor.transpose(spread[:, i, :], gate_cols[:, g, i : i + 1].to_broadcast([P, P]), identity[:])
             nc.scalar.copy(
@@ -137,207 +107,125 @@ def tile_moe_pre_glu_gelu_kernel(
                 in_=spread[:].rearrange("p i n -> p n i"),
             )
 
-        def load_weights(w, e, width, tag, bufs):
-            t = raw.tile([P, PACK, width], F32, name=tag, tag=tag, bufs=bufs)
-            nc.sync.dma_start(t[:], w[e].rearrange("(p j) c -> p j c", j=PACK))
-            return t
+        first_raw = []
 
-        loaded = {}
-
-        def load(kind, i):
-            if (kind, i) in loaded:
-                return loaded[kind, i]
-            if kind == "x":
-                if X_SPLIT and i == 0:
-                    nc.sync.dma_start(x_rows[i][:, 0 : T // 2], x_view[:, i, 0 : T // 2])
-                    nc.scalar.dma_start(x_rows[i][:, T // 2 : T], x_view[:, i, T // 2 : T])
-                elif i in X_ON_ACT:
-                    nc.scalar.dma_start(x_rows[i][:], x_view[:, i, :])
-                else:
-                    nc.sync.dma_start(x_rows[i][:], x_view[:, i, :])
-                loaded[kind, i] = x_rows[i]
-            elif kind == "a":
-                loaded[kind, i] = load_weights(w1, i, H, "w_raw", RAW_BUFS)
-            elif kind == "b":
-                loaded[kind, i] = load_weights(w3, i, H, "w_raw", RAW_BUFS)
-            else:
-                t = raw.tile([P, CE, PACK, N], F32, name="w2_raw", tag="w2_raw", bufs=C_BUFS)
-                if PAIRS:
-                    rows = w2[i].rearrange("(c t r) n -> r c t n", t=PACK, r=2)
-                    for r in range(2):
-                        nc.sync.dma_start(t[r:P:2, 0, :, :], rows[r])
-                else:
-                    nc.sync.dma_start(
-                        t[:].rearrange("p e j n -> p e (j n)"),
-                        w2[i : i + CE].rearrange("e (p j) n -> p e (j n)", j=PACK),
-                    )
-                for k in range(CE):
-                    loaded[kind, i + k] = t
-            return loaded[kind, i]
+        def load_first_up_to(count):
+            while len(first_raw) < count:
+                e, which = divmod(len(first_raw), 2)
+                tile = raw.tile([P, PACK, H], F32, name="w_raw", tag="w_raw")
+                nc.sync.dma_start(tile[:], (w1, w3)[which][e].rearrange("(p j) c -> p j c", j=PACK))
+                first_raw.append(tile)
 
         nc.sync.dma_start(offs_sb[:], offs)
-        for item in HEAD.split():
-            load(item[0], int(item[1:]))
+        x_view = xT.rearrange("(p j) t -> p j t", j=PACK)
+        for j in range(PACK):
+            load_first_up_to(2 * j - 1)
+            nc.sync.dma_start(x_rows[j][:], x_view[:, j, :])
 
-        x_codes = {}
+        gather_at = {sum(GATHERS[:g]) // C: count for g, count in enumerate(GATHERS)}
+        gated = {}
 
-        def gather_group(g):
-            s0, n = starts[g], GROUPS[g]
-            xg = work.tile([P, PACK, n], F32, name="xg", tag="xg", bufs=XG_BUFS)
+        def gather_tokens(e):
+            start, count = e * C, gather_at[e]
+            xg = work.tile([P, PACK, count], F32, name="xg", tag="xg", bufs=4)
             for j in range(PACK):
                 nc.vector.tensor_tensor(
                     out=xg[:, j, :],
-                    in0=x_rows[j][:].indirect(offs_sb[:, s0 // 16 : (s0 + n) // 16]),
-                    in1=gate_all[:, s0 : s0 + n],
+                    in0=x_rows[j][:].indirect(entries(offs_sb, start, count)),
+                    in1=gate_all[:, start : start + count],
                     op=MULT,
                 )
-            return xg
-
-        gathered = {}
-
-        tokens_q = {}
+            for k in range(count // C):
+                gated[e + k] = xg[:, :, k * C : (k + 1) * C]
 
         def quantize_tokens(e):
-            if e in tokens_q:
-                return tokens_q[e]
-            g = max(i for i in range(len(GROUPS)) if starts[i] <= e * C)
-            c0 = e * C - starts[g]
-            n = min(XW, GROUPS[g] - c0)
-            xb = work.tile([P, n * PACK], BF16, name="xb", tag="xb", bufs=XB_BUFS, align_bytes=64)
-            interleave("scalar" if e in X_ON_SCALAR else "vector", xb[:], gathered[g][:, :, c0 : c0 + n])
-            xc = work.tile([P, n], U32, name="xc", tag="xc", bufs=XC_BUFS, align_bytes=64)
-            xs = work.tile([P, n], U8, name="xs", tag="xs", bufs=XC_BUFS, align_bytes=64)
-            quantize(xc[:], xs[:], xb[:])
-            for i in range(n // C):
-                tokens_q[e + i] = (xc[:, i * C : (i + 1) * C], xs[:, i * C : (i + 1) * C])
-            return tokens_q[e]
+            xb = work.tile([P, C * PACK], BF16, name="xb", tag="xb", align_bytes=64)
+            round_rows(True, xb[:], gated[e])
+            return quantize(xb[:], C, "x", 6)
 
-        def quantize_first(w_raw, engine, first=False):
-            if first:
+        def quantize_first(number, on_vector):
+            if number == 0:
                 wb = keep.tile([P, H * PACK], BF16, name="wb0", tag="first", align_bytes=64)
             else:
-                wb = work.tile([P, H * PACK], BF16, name="wb", tag="wb", bufs=WB_BUFS, align_bytes=64)
-            interleave_permuted(engine, wb[:], w_raw[:])
-            wc = work.tile([P, H], U32, name="wc", tag="wc", bufs=WC_BUFS, align_bytes=64)
-            ws = work.tile([P, H], U8, name="ws", tag="ws", bufs=WC_BUFS, align_bytes=64)
-            quantize(wc[:], ws[:], wb[:])
-            return wc, ws
+                wb = work.tile([P, H * PACK], BF16, name="wb", tag="wb", bufs=4, align_bytes=64)
+            round_rows_permuted(on_vector, wb[:], first_raw[number][:])
+            return quantize(wb[:], H, "w", 4)
 
-        def quantize_both(w1_raw, w3_raw, engine, first):
-            if first:
-                wb = keep.tile([P, 2, H * PACK], BF16, name="wb0", tag="first", align_bytes=64)
-            else:
-                wb = work.tile([P, 2, H * PACK], BF16, name="wb", tag="wb", bufs=(WB_BUFS + 1) // 2, align_bytes=64)
-            interleave_permuted("scalar", wb[:, 0, :], w1_raw[:])
-            interleave_permuted(engine, wb[:, 1, :], w3_raw[:])
-            wc = work.tile([P, 2 * H], U32, name="wc", tag="wc", bufs=WC_BUFS // 2, align_bytes=64)
-            ws = work.tile([P, 2 * H], U8, name="ws", tag="ws", bufs=WC_BUFS // 2, align_bytes=64)
-            quantize(wc[:], ws[:], wb[:].rearrange("p a b -> p (a b)"))
-            return (wc[:, 0:H], ws[:, 0:H]), (wc[:, H : 2 * H], ws[:, H : 2 * H])
-
-        def prepare(e):
-            for g in range(len(GROUPS)):
-                if g not in gathered and starts[g] <= (e + GATHER_AHEAD) * C:
-                    gathered[g] = gather_group(g)
+        def prepare_first(e):
+            if e in gather_at:
+                gather_tokens(e)
             x_q = quantize_tokens(e)
-            w1_raw = load("a", e)
-            w3_raw = load("b", e)
-            if 0 <= e + C_AHEAD < E and (e + C_AHEAD) % CE == 0:
-                load("c", e + C_AHEAD)
+            load_first_up_to(2 * e + 2)
             if e == E // 2:
                 nc.sync.dma_start(pos1_sb[:], pos1)
                 nc.sync.dma_start(pos2_sb[:], pos2)
-            if WPAIR:
-                w1_q, w3_q = quantize_both(w1_raw, w3_raw, "vector" if e in W3_ON_VECTOR else "scalar", e == 0)
-                return x_q, w1_q, w3_q
-            w1_q = quantize_first(w1_raw, "scalar", e == 0)
-            w3_q = quantize_first(w3_raw, "vector" if e in W3_ON_VECTOR else "scalar")
-            return x_q, w1_q, w3_q
+            return x_q, quantize_first(2 * e, False), quantize_first(2 * e + 1, e >= W3_ON_VECTOR_FROM)
 
         def prepare_second(e):
-            if e in second:
-                return second[e]
-            w2_raw = load("c", e)
-            w2b = work.tile([P, CE * N * PACK], BF16, name="w2b", tag="w2b", align_bytes=64)
-            for k in range(CE):
-                interleave(
-                    "scalar" if e in W2_ON_SCALAR else "vector",
-                    w2b[:, k * N * PACK : (k + 1) * N * PACK],
-                    w2_raw[:, k, :, :],
-                )
-            w2c = work.tile([P, CE * N], U32, name="w2c", tag="w2c", align_bytes=64)
-            w2s = work.tile([P, CE * N], U8, name="w2s", tag="w2s", align_bytes=64)
-            quantize(w2c[:], w2s[:], w2b[:])
-            for k in range(CE):
-                second[e + k] = (w2c[:, k * N : (k + 1) * N], w2s[:, k * N : (k + 1) * N])
-            return second[e]
+            w2_raw = raw.tile([P, PAIR, PACK, N], F32, name="w2_raw", tag="w2_raw", bufs=3)
+            nc.sync.dma_start(
+                w2_raw[:].rearrange("p e j n -> p e (j n)"),
+                w2[e : e + PAIR].rearrange("e (p j) n -> p e (j n)", j=PACK),
+            )
+            w2b = work.tile([P, PAIR * N * PACK], BF16, name="w2b", tag="w2b", align_bytes=64)
+            for k in range(PAIR):
+                round_rows(e < W2_ON_SCALAR_FROM, w2b[:, k * N * PACK : (k + 1) * N * PACK], w2_raw[:, k, :, :])
+            return quantize(w2b[:], PAIR * N, "w2", 3)
 
         def first_layer(x_q, w1_q, w3_q):
-            xc, xs = x_q
-            hb = work.tile([P, C, PACK], BF16, name="hb", tag="hb", bufs=HB_BUFS, align_bytes=64)
-            for half in range(C // HALF):
-                cols = slice(half * HALF, (half + 1) * HALF)
-                a_ps = psum.tile([P, PACK, HALF], F32, name="a_ps", tag="a_ps", bufs=PS_A)
-                b_ps = psum.tile([P, PACK, HALF], F32, name="b_ps", tag="b_ps", bufs=PS_B)
-                for acc, (wc, ws) in ((a_ps, w1_q), (b_ps, w3_q)):
+            hb = work.tile([P, C, PACK], BF16, name="hb", tag="hb", bufs=2, align_bytes=64)
+            for s0 in range(0, C, HALF):
+                a_ps = psum.tile([P, PACK, HALF], F32, name="a_ps", tag="a_ps")
+                b_ps = psum.tile([P, PACK, HALF], F32, name="b_ps", tag="b_ps")
+                for acc, w_q in ((a_ps, w1_q), (b_ps, w3_q)):
                     for t in range(PACK):
-                        m_cols = slice(t * P, (t + 1) * P)
-                        product(acc[:, t, :], wc[:, m_cols], ws[:, m_cols], xc[:, cols], xs[:, cols])
-                act = work.tile([P, HALF, PACK], F32, name="act", tag="act", bufs=ACT_BUFS)
+                        product(acc[:, t, :], columns(w_q, t * P, P), columns(x_q, s0, HALF))
+                act = work.tile([P, HALF, PACK], F32, name="act", tag="act", bufs=4)
                 nc.scalar.activation(out=act[:], in_=a_ps[:].rearrange("p t s -> p s t"), func=GELU)
                 nc.vector.tensor_tensor(
-                    out=hb[:, cols, :], in0=b_ps[:].rearrange("p t s -> p s t"), in1=act[:], op=MULT
+                    out=hb[:, s0 : s0 + HALF, :], in0=b_ps[:].rearrange("p t s -> p s t"), in1=act[:], op=MULT
                 )
             return hb
 
-        def second_layer(e, hb, w2_q):
-            hc = work.tile([P, C], U32, name="hc", tag="hc", bufs=HC_BUFS, align_bytes=64)
-            hs = work.tile([P, C], U8, name="hs", tag="hs", bufs=HC_BUFS, align_bytes=64)
-            quantize(hc[:], hs[:], hb[:].rearrange("p s t -> p (s t)"))
-            if YPAIR and e < YPAIR:
-                if e % 2 == 0:
-                    y_banks[e // 2] = psum_y.tile([P, 2 * C], F32, name="y_ps", tag="y_ps")
-                y_ps = y_banks[e // 2]
-                product(y_ps[:, (e % 2) * C : (e % 2 + 1) * C], w2_q[0], w2_q[1], hc[:], hs[:])
-                if e % 2 == 1:
-                    copy_on("vector" if e in Y_ON_VECTOR else "scalar", y_all[:, (e - 1) * C : (e + 1) * C], y_ps[:])
-                return
-            y_ps = psum_y.tile([P, C], F32, name="y_ps", tag="y_ps")
-            product(y_ps[:], w2_q[0], w2_q[1], hc[:], hs[:])
-            copy_on("vector" if e in Y_ON_VECTOR else "scalar", y_all[:, e * C : (e + 1) * C], y_ps[:])
-
         y_banks = {}
-        ready = {}
-        hidden = {}
-        second = {}
-        for step in range(E + LAG2):
-            if step < E:
-                ready[step] = prepare(step)
-            e = step - LAGW
-            if 0 <= e < E:
-                second[e] = prepare_second(e)
-            e = step - LAG1
-            if 0 <= e < E:
-                hidden[e] = first_layer(*ready[e])
-            e = step - LAG2
-            if 0 <= e < E:
-                second_layer(e, hidden[e], second[e])
 
-        first = keep.tile([P, T], F32, name="first_results")
-        t0 = 0
-        for width in FIRST_PIECES:
+        def second_layer(e, hb, w2_pair):
+            h_q = quantize(hb[:].rearrange("p s t -> p (s t)"), C, "h", 2)
+            together = PAIR if e < E - PAIR else 1
+            place = e % together
+            if place == 0:
+                y_banks[e] = psum_y.tile([P, together * C], F32, name="y_ps", tag="y_ps")
+            y_ps = y_banks[e - place]
+            product(y_ps[:, place * C : (place + 1) * C], columns(w2_pair, (e % PAIR) * N, N), columns(h_q, 0, C))
+            if place == together - 1:
+                copy_on(e == E - 1, y_all[:, (e - place) * C : (e + 1) * C], y_ps[:])
+
+        operands, w2_pairs, hidden = {}, {}, {}
+        for step in range(E + SECOND_LAYER_LAG):
+            if step < E:
+                operands[step] = prepare_first(step)
+            e = step - W2_LAG
+            if 0 <= e < E and e % PAIR == 0:
+                w2_pairs[e] = prepare_second(e)
+            e = step - FIRST_LAYER_LAG
+            if 0 <= e < E:
+                hidden[e] = first_layer(*operands[e])
+            e = step - SECOND_LAYER_LAG
+            if 0 <= e < E:
+                second_layer(e, hidden[e], w2_pairs[e - e % PAIR])
+
+        first_results = keep.tile([P, T], F32, name="first_results")
+        for t0 in range(0, T, T // 2):
             nc.vector.tensor_copy(
-                out=first[:, t0 : t0 + width], in_=y_all[:].indirect(pos1_sb[:, t0 // 16 : (t0 + width) // 16])
+                out=first_results[:, t0 : t0 + T // 2], in_=y_all[:].indirect(entries(pos1_sb, t0, T // 2))
             )
-            t0 += width
-        t0 = 0
-        for i, width in enumerate(OUT_PIECES):
+        for i, width in enumerate(STORE_WIDTHS):
+            t0 = sum(STORE_WIDTHS[:i])
             total = keep.tile([P, width], F32, name="total%d" % i)
             nc.vector.tensor_tensor(
                 out=total[:],
-                in0=y_all[:].indirect(pos2_sb[:, t0 // 16 : (t0 + width) // 16]),
-                in1=first[:, t0 : t0 + width],
+                in0=y_all[:].indirect(entries(pos2_sb, t0, width)),
+                in1=first_results[:, t0 : t0 + width],
                 op=ADD,
             )
             nc.sync.dma_start(out[:, t0 : t0 + width], total[:])
-            t0 += width

from contextlib import ExitStack

import concourse.mybir as mybir
from concourse.masks import make_identity

K, T, E, C, H, N = 512, 1280, 10, 256, 512, 128
S = E * C
FLOPS = 2 * S * (2 * K * H + H * N)
BYTES = 4 * (K * T + 2 * E * K * H + E * H * N + S + N * T) + 2 * 128 * (S + 2 * T) // 16

F32 = mybir.dt.float32
BF16 = mybir.dt.bfloat16
U32 = mybir.dt.uint32
U16 = mybir.dt.uint16
U8 = mybir.dt.uint8
FP8X4 = mybir.dt.float8_e4m3fn_x4
MULT = mybir.AluOpType.mult
ADD = mybir.AluOpType.add
GELU = mybir.ActivationFunctionType.Gelu_apprx_tanh

P = 128
PACK = 4
LIST = 16
BANK = 512
HALF = BANK // PACK
PAIR = 2

GATHERS = (C, C) + (PAIR * C,) * ((E - 2) // PAIR)
W3_ON_VECTOR_FROM = E - 2
W2_ON_SCALAR_FROM = PAIR
FIRST_LAYER_LAG, W2_LAG, SECOND_LAYER_LAG = 2, 3, 4
STORE_WIDTHS = (640, 512, 128)


def tile_moe_pre_glu_gelu_kernel(
    tc, xT, w1, w3, w2, gate, offs, pos1, pos2, out
):
    nc = tc.nc

    def copy_on(on_vector, dst, src):
        if on_vector:
            nc.vector.tensor_copy(out=dst, in_=src)
        else:
            nc.scalar.copy(out=dst, in_=src)

    def round_rows(on_vector, dst, src):
        copy_on(
            on_vector,
            dst.rearrange("p (c i u v) -> p c u i v", i=4, u=2, v=2),
            src.rearrange("p (u v) (c i) -> p c u i v", i=4, v=2),
        )

    def round_rows_permuted(on_vector, dst, src):
        copy_on(
            on_vector,
            dst.rearrange("p (t m u v) -> p m u t v", t=PACK, u=2, v=2),
            src.rearrange("p (u v) (m t) -> p m u t v", t=PACK, v=2),
        )

    def product(acc, stationary, moving):
        nc.tensor.matmul_mx(
            out=acc,
            lhsT=stationary[0].bitcast(FP8X4),
            lhsT_scale=stationary[1],
            rhs=moving[0].bitcast(FP8X4),
            rhs_scale=moving[1],
            start=True,
            stop=True,
        )

    def columns(operand, start, width):
        return operand[0][:, start : start + width], operand[1][:, start : start + width]

    def entries(list_sb, start, count):
        return list_sb[:, start // LIST : (start + count) // LIST]

    with ExitStack() as ctx:
        keep = ctx.enter_context(tc.tile_pool(name="keep", bufs=1))
        raw = ctx.enter_context(tc.tile_pool(name="raw", bufs=7))
        work = ctx.enter_context(tc.tile_pool(name="work", bufs=3))
        psum = ctx.enter_context(tc.psum_pool(name="psum", bufs=3))
        psum_y = ctx.enter_context(tc.psum_pool(name="psum_y", bufs=2))

        def quantize(values, width, tag, bufs):
            codes = work.tile([P, width], U32, name=tag + "c", tag=tag + "c", bufs=bufs, align_bytes=64)
            scales = work.tile([P, width], U8, name=tag + "s", tag=tag + "s", bufs=bufs, align_bytes=64)
            nc.vector.quantize_mx(out=codes[:].bitcast(FP8X4), scales=scales[:], in_=values)
            return codes, scales

        offs_sb = keep.tile([P, S // LIST], U16, name="offs_sb")
        pos1_sb = keep.tile([P, T // LIST], U16, name="pos1_sb")
        pos2_sb = keep.tile([P, T // LIST], U16, name="pos2_sb")
        x_rows = [keep.tile([P, T], F32, name="x_row%d" % j) for j in range(PACK)]
        y_all = keep.tile([P, S], F32, name="y_all")

        gate_all = keep.tile([P, S], F32, name="gate_all")
        gate_cols = keep.tile([P, S // BANK, PACK], F32, name="gate_cols", tag="first", align_bytes=64)
        identity = keep.tile([P, P], F32, name="identity")
        make_identity(nc, identity[:])
        nc.sync.dma_start(gate_cols[:], gate[0].rearrange("(g n i) -> n g i", n=P, i=PACK))
        for g in range(S // BANK):
            spread = psum.tile([P, PACK, P], F32, name="spread", tag=("a_ps", "b_ps")[g % 2])
            for i in range(PACK):
                nc.tensor.transpose(spread[:, i, :], gate_cols[:, g, i : i + 1].to_broadcast([P, P]), identity[:])
            nc.scalar.copy(
                out=gate_all[:, g * BANK : (g + 1) * BANK].rearrange("p (n i) -> p n i", i=PACK),
                in_=spread[:].rearrange("p i n -> p n i"),
            )

        first_raw = []

        def load_first_up_to(count):
            while len(first_raw) < count:
                e, which = divmod(len(first_raw), 2)
                tile = raw.tile([P, PACK, H], F32, name="w_raw", tag="w_raw")
                nc.sync.dma_start(tile[:], (w1, w3)[which][e].rearrange("(p j) c -> p j c", j=PACK))
                first_raw.append(tile)

        nc.sync.dma_start(offs_sb[:], offs)
        x_view = xT.rearrange("(p j) t -> p j t", j=PACK)
        for j in range(PACK):
            load_first_up_to(2 * j - 1)
            nc.sync.dma_start(x_rows[j][:], x_view[:, j, :])

        gather_at = {sum(GATHERS[:g]) // C: count for g, count in enumerate(GATHERS)}
        gated = {}

        def gather_tokens(e):
            start, count = e * C, gather_at[e]
            xg = work.tile([P, PACK, count], F32, name="xg", tag="xg", bufs=4)
            for j in range(PACK):
                nc.vector.tensor_tensor(
                    out=xg[:, j, :],
                    in0=x_rows[j][:].indirect(entries(offs_sb, start, count)),
                    in1=gate_all[:, start : start + count],
                    op=MULT,
                )
            for k in range(count // C):
                gated[e + k] = xg[:, :, k * C : (k + 1) * C]

        def quantize_tokens(e):
            xb = work.tile([P, C * PACK], BF16, name="xb", tag="xb", align_bytes=64)
            round_rows(True, xb[:], gated[e])
            return quantize(xb[:], C, "x", 6)

        def quantize_first(number, on_vector):
            if number == 0:
                wb = keep.tile([P, H * PACK], BF16, name="wb0", tag="first", align_bytes=64)
            else:
                wb = work.tile([P, H * PACK], BF16, name="wb", tag="wb", bufs=4, align_bytes=64)
            round_rows_permuted(on_vector, wb[:], first_raw[number][:])
            return quantize(wb[:], H, "w", 4)

        def prepare_first(e):
            if e in gather_at:
                gather_tokens(e)
            x_q = quantize_tokens(e)
            load_first_up_to(2 * e + 2)
            if e == E // 2:
                nc.sync.dma_start(pos1_sb[:], pos1)
                nc.sync.dma_start(pos2_sb[:], pos2)
            return x_q, quantize_first(2 * e, False), quantize_first(2 * e + 1, e >= W3_ON_VECTOR_FROM)

        def prepare_second(e):
            w2_raw = raw.tile([P, PAIR, PACK, N], F32, name="w2_raw", tag="w2_raw", bufs=3)
            nc.sync.dma_start(
                w2_raw[:].rearrange("p e j n -> p e (j n)"),
                w2[e : e + PAIR].rearrange("e (p j) n -> p e (j n)", j=PACK),
            )
            w2b = work.tile([P, PAIR * N * PACK], BF16, name="w2b", tag="w2b", align_bytes=64)
            for k in range(PAIR):
                round_rows(e < W2_ON_SCALAR_FROM, w2b[:, k * N * PACK : (k + 1) * N * PACK], w2_raw[:, k, :, :])
            return quantize(w2b[:], PAIR * N, "w2", 3)

        def first_layer(x_q, w1_q, w3_q):
            hb = work.tile([P, C, PACK], BF16, name="hb", tag="hb", bufs=2, align_bytes=64)
            for s0 in range(0, C, HALF):
                a_ps = psum.tile([P, PACK, HALF], F32, name="a_ps", tag="a_ps")
                b_ps = psum.tile([P, PACK, HALF], F32, name="b_ps", tag="b_ps")
                for acc, w_q in ((a_ps, w1_q), (b_ps, w3_q)):
                    for t in range(PACK):
                        product(acc[:, t, :], columns(w_q, t * P, P), columns(x_q, s0, HALF))
                act = work.tile([P, HALF, PACK], F32, name="act", tag="act", bufs=4)
                nc.scalar.activation(out=act[:], in_=a_ps[:].rearrange("p t s -> p s t"), func=GELU)
                nc.vector.tensor_tensor(
                    out=hb[:, s0 : s0 + HALF, :], in0=b_ps[:].rearrange("p t s -> p s t"), in1=act[:], op=MULT
                )
            return hb

        y_banks = {}

        def second_layer(e, hb, w2_pair):
            h_q = quantize(hb[:].rearrange("p s t -> p (s t)"), C, "h", 2)
            together = PAIR if e < E - PAIR else 1
            place = e % together
            if place == 0:
                y_banks[e] = psum_y.tile([P, together * C], F32, name="y_ps", tag="y_ps")
            y_ps = y_banks[e - place]
            product(y_ps[:, place * C : (place + 1) * C], columns(w2_pair, (e % PAIR) * N, N), columns(h_q, 0, C))
            if place == together - 1:
                copy_on(e == E - 1, y_all[:, (e - place) * C : (e + 1) * C], y_ps[:])

        operands, w2_pairs, hidden = {}, {}, {}
        for step in range(E + SECOND_LAYER_LAG):
            if step < E:
                operands[step] = prepare_first(step)
            e = step - W2_LAG
            if 0 <= e < E and e % PAIR == 0:
                w2_pairs[e] = prepare_second(e)
            e = step - FIRST_LAYER_LAG
            if 0 <= e < E:
                hidden[e] = first_layer(*operands[e])
            e = step - SECOND_LAYER_LAG
            if 0 <= e < E:
                second_layer(e, hidden[e], w2_pairs[e - e % PAIR])

        first_results = keep.tile([P, T], F32, name="first_results")
        for t0 in range(0, T, T // 2):
            nc.vector.tensor_copy(
                out=first_results[:, t0 : t0 + T // 2], in_=y_all[:].indirect(entries(pos1_sb, t0, T // 2))
            )
        for i, width in enumerate(STORE_WIDTHS):
            t0 = sum(STORE_WIDTHS[:i])
            total = keep.tile([P, width], F32, name="total%d" % i)
            nc.vector.tensor_tensor(
                out=total[:],
                in0=y_all[:].indirect(entries(pos2_sb, t0, width)),
                in1=first_results[:, t0 : t0 + width],
                op=ADD,
            )
            nc.sync.dma_start(out[:, t0 : t0 + width], total[:])
